import numpy as np
import ml_dtypes


def mxq(x, axis, fmt="e4m3"):
    dtype, down = {"e4m3": (ml_dtypes.float8_e4m3fn, 7), "e5m2": (ml_dtypes.float8_e5m2, 14)}[fmt]
    v = np.moveaxis(np.asarray(x, np.float32).astype(ml_dtypes.bfloat16).astype(np.float64), axis, -1)
    blocks = v.reshape(v.shape[:-1] + (-1, 32))
    amax = np.abs(blocks).max(-1, keepdims=True)
    byte = np.maximum(np.where(amax > 0, np.frexp(amax)[1] - 1 + 127, 0) - down, 1)
    scale = np.exp2(byte - 127.0)
    codes = (blocks / scale).astype(np.float32).astype(dtype).astype(np.float64)
    return np.moveaxis((codes * scale).reshape(v.shape), -1, axis)


WIDE = False


def mx_kscale(k):
    if not WIDE:
        return np.ones(k)
    levels = np.array([30, -30])
    if k % 512:
        return np.exp2(np.random.permutation(np.resize(levels, k // 32))).repeat(32)
    a = np.empty((k // 512, 16))
    for p in range(k // 512):
        a[p, :8] = np.random.permutation(np.resize(levels, 8))
        for g in range(8):
            far = levels[np.abs(levels - a[p, g]) >= 10]
            a[p, g + 8] = far[np.random.randint(len(far))]
    return np.exp2(a.ravel()).repeat(32)


def f64(x):
    return np.asarray(x).astype(np.float64)


def striped(idx):
    return np.tile(np.asarray(idx).reshape(-1, 16).T, (8, 1)).astype(np.uint16)


def unstriped(offs):
    return offs[:16].T.reshape(-1).astype(np.int64)


E2M1 = np.array([0.0, 0.5, 1.0, 1.5, 2.0, 3.0, 4.0, 6.0, -0.0, -0.5, -1.0, -1.5, -2.0, -3.0, -4.0, -6.0])


def pack_weight(w, fmt):
    k, n = w.shape
    w = f64(np.asarray(w, np.float32).astype(ml_dtypes.bfloat16)).reshape(k // 32, 32, n)
    amax = np.abs(w).max(1)
    if fmt in ("e4m3", "e5m2"):
        byte = np.frexp(amax)[1] - 1 + 127 - (7 if fmt == "e4m3" else 14)
    else:
        mant, ex = np.frexp(amax / 6.0)
        byte = np.where(mant > 0.5, ex, ex - 1) + 127
    byte = np.clip(np.where(amax > 0, byte, 1), 1, 254)
    scaled = (w * np.exp2(127.0 - byte)[:, None, :]).reshape(k, n).astype(np.float32)
    by_word = np.ascontiguousarray(scaled.reshape(k // 512, 128, 4, n).transpose(0, 1, 3, 2))
    if fmt in ("e4m3", "e5m2"):
        words = by_word.astype(ml_dtypes.float8_e4m3fn if fmt == "e4m3" else ml_dtypes.float8_e5m2).view(np.uint8)
    else:
        c = by_word.astype(ml_dtypes.float4_e2m1fn).view(np.uint8) & 0xF
        words = (c[..., 0::2] | (c[..., 1::2] << 4)).reshape(k // 512, 128, 2 * n)
    return np.ascontiguousarray(words), np.ascontiguousarray(byte.astype(np.uint8).reshape(k // 512, 16, n))


def unpack_weight(words, scales, fmt):
    g, _, n = scales.shape
    words = np.ascontiguousarray(words).reshape(g, 128, n, -1)
    if fmt in ("e4m3", "e5m2"):
        vals = words.view(ml_dtypes.float8_e4m3fn if fmt == "e4m3" else ml_dtypes.float8_e5m2).astype(np.float64)
    else:
        nib = np.empty((g, 128, n, 4), np.uint8)
        nib[..., 0::2] = words & 0xF
        nib[..., 1::2] = words >> 4
        vals = E2M1[nib]
    vals = vals * np.repeat(np.exp2(scales.astype(np.float64) - 127.0), 8, axis=1)[..., None]
    return vals.transpose(0, 1, 3, 2).reshape(g * 512, n)


K, T, J, N = 1024, 1024, 256, 256


def setup_inputs():
    n = np.random.standard_normal
    idx = np.random.permutation(T)[:J]
    idx2 = np.random.permutation(T)[:J]
    fk = mx_kscale(K)
    xtp = pack_weight(n((K, T)) * np.random.uniform(0.4, 1.6, (1, T)) / fk[:, None], "e5m2")
    wap = pack_weight(n((K, N)) * 1 / np.sqrt(K) * fk[:, None], "e4m3")
    return {
        "xt_words": xtp[0],
        "xt_scales": xtp[1],
        "wa_words": wap[0],
        "wa_scales": wap[1],
        "wb": (n((K, N)) * 1 / np.sqrt(K) * fk[:, None]).astype(np.float32),
        "bi": (np.random.uniform(-0.6, 0.6, (1, N))).astype(np.float32),
        "gm": (np.random.uniform(0.5, 2.0, (1, N))).astype(np.float32),
        "offs": striped(idx),
        "offs2": striped(idx2),
    }


def reference(xt_words, xt_scales, wa_words, wa_scales, wb, bi, gm, offs, offs2):
    idx = unstriped(offs)
    idx2 = unstriped(offs2)
    xtu = unpack_weight(xt_words, xt_scales, "e5m2")
    wau = unpack_weight(wa_words, wa_scales, "e4m3")
    xtidxg = xtu[:, idx]
    a = xtidxg.T @ wau
    xtidx2g = xtu[:, idx2]
    wbq = mxq(f64(wb), 0, "e4m3")
    b0 = xtidx2g.T @ wbq
    b2 = b0 + f64(bi)
    d1 = np.mean(np.square(a - b2), axis=1, keepdims=True)
    y = a * f64(gm) / (0.4 + d1)
    return y

@@ -1,0 +1,173 @@
+import math
+from contextlib import ExitStack
+
+import concourse.mybir as mybir
+
+K, T, J, N = 1024, 1024, 256, 256
+FLOPS = 2 * 2 * K * J * N
+
+F32 = mybir.dt.float32
+BF16 = mybir.dt.bfloat16
+I32 = mybir.dt.int32
+U32 = mybir.dt.uint32
+U16 = mybir.dt.uint16
+U8 = mybir.dt.uint8
+E4M3X4 = mybir.dt.float8_e4m3fn_x4
+E5M2X4 = mybir.dt.float8_e5m2_x4
+ALU = mybir.AluOpType
+ACT = mybir.ActivationFunctionType
+
+P = 128
+PACK = 4
+K_PASS = P * PACK
+PASSES = K // K_PASS
+QUADS = 4
+QUAD = P // QUADS
+ROWS = 4
+SLOT_TILES = J // P
+GAP_FLOOR = 0.4
+VECTOR_COLS = 144
+
+
+def round_and_interleave(copy, grouped, raw, c0, c1):
+    copy(
+        grouped[:, c0:c1, :].rearrange("p (c i) t -> p c t i", i=4),
+        raw[:, :, c0:c1].rearrange("p t (c i) -> p c t i", i=4),
+    )
+
+
+def tile_list_rows_twotokens_bygapsize_kernel(tc, xt_words, xt_scales, wa_words, wa_scales, wb, bi, gm, offs, offs2, out):
+    nc = tc.nc
+    with ExitStack() as ctx:
+        sb = ctx.enter_context(tc.tile_pool(name="sb", bufs=1))
+        late = ctx.enter_context(tc.tile_pool(name="late", bufs=1))
+        ps = ctx.enter_context(tc.psum_pool(name="ps", bufs=1))
+
+        lists = [sb.tile([P, J // 16], U16, name="list%d" % s) for s in range(2)]
+        ramp = late.tile([P, QUAD], F32, name="ramp", align_bytes=64, offset=4 * T - 64)
+        ramp_t = late.tile([P, QUAD], F32, name="ramp_t", align_bytes=64, offset=4 * T + 4 * PACK * N)
+        x_words = [
+            sb.tile([P, T], U32, name="x_words0", align_bytes=64),
+            late.tile([P, T], U32, name="x_words1", align_bytes=64, offset=0),
+        ]
+        x_scales = sb.tile([P, T], U8, name="x_scales", align_bytes=64)
+        wa_codes = late.tile([P, PASSES, N], U32, name="wa_codes", align_bytes=64, offset=4 * T + 64 + 4 * PACK * N)
+        wa_plane = sb.tile([P, PASSES * N], U8, name="wa_plane", align_bytes=64)
+        wb_raw = [
+            sb.tile([P, PACK, N], F32, name="wb_raw0"),
+            late.tile([P, PACK, N], F32, name="wb_raw1", align_bytes=64, offset=4 * T + 64),
+        ]
+        wb_grouped = [sb.tile([P, N, PACK], BF16, name="wb_grouped%d" % z, align_bytes=64) for z in range(PASSES)]
+        wb_codes = [sb.tile([P, N], U32, name="wb_codes%d" % z, align_bytes=64) for z in range(PASSES)]
+        wb_plane = [sb.tile([P, N], U8, name="wb_plane%d" % z, align_bytes=64) for z in range(PASSES)]
+        picked_scales = sb.tile([P, 2 * J], U8, name="picked_scales", align_bytes=64)
+        moved_scales = sb.tile([P, 2 * J], U8, name="moved_scales", align_bytes=64)
+        picked = [[sb.tile([P, J], U32, name="picked%d%d" % (s, z), align_bytes=64) for z in range(PASSES)] for s in range(2)]
+        cols = [late.tile([P, N // P], F32, name="cols%d" % v, offset=4 * T + 32 * v) for v in range(2)]
+        rows = sb.tile([P, 2, N], F32, name="rows")
+        ident = sb.tile([P, P], F32, name="ident")
+        ones = sb.tile([P, QUAD], F32, name="ones")
+        gap = sb.tile([P, SLOT_TILES, N + 1], F32, name="gap")
+
+        nc.vector.memset(x_scales[:].bitcast(I32), 0)
+        nc.sync.dma_start(lists[0][:], offs)
+        nc.scalar.dma_start(x_words[0][:].bitcast(I32), xt_words[0].rearrange("p n t -> p (n t)").bitcast(I32))
+        nc.sync.dma_start(lists[1][:], offs2)
+        nc.scalar.dma_start(wb_raw[0][:], wb[0:K_PASS, :].rearrange("(p t) n -> p t n", t=PACK))
+        xs_rows = xt_scales.bitcast(I32)
+        for q in range(QUADS):
+            nc.sync.dma_start(
+                x_scales[QUAD * q : QUAD * q + PASSES * ROWS, :].bitcast(I32), xs_rows[:, ROWS * q : ROWS * (q + 1), :]
+            )
+        nc.vector.memset(ones[:], 1.0)
+        nc.scalar.activation(gap[:, :, N], ones[:, 0:SLOT_TILES], ACT.Copy, scale=math.sqrt(GAP_FLOOR * N))
+        nc.vector.tensor_tensor_scan(ramp[:], ones[:], ones[:], 0.0, ALU.mult, ALU.add)
+        nc.vector.memset(ident[:], 0.0)
+        nc.vector.transpose(ramp_t[:], ramp[:])
+        for q in range(QUADS):
+            quad = slice(QUAD * q, QUAD * (q + 1))
+            nc.vector.tensor_tensor(ident[quad, quad], ramp[quad, :], ramp_t[quad, :], ALU.is_equal)
+        nc.scalar.dma_start(x_words[1][:].bitcast(I32), xt_words[1].rearrange("p n t -> p (n t)").bitcast(I32))
+        for v, vec in enumerate((bi, gm)):
+            nc.scalar.dma_start(cols[v][:], vec.rearrange("o (p c) -> (o p) c", c=N // P))
+        nc.scalar.dma_start(wb_raw[1][:], wb[K_PASS:K, :].rearrange("(p t) n -> p t n", t=PACK))
+        nc.scalar.dma_start(wa_codes[:].bitcast(I32), wa_words.rearrange("z p n t -> p z (n t)").bitcast(I32))
+
+        nc.vector.memset(wa_plane[:].bitcast(I32), 0)
+        nc.vector.memset(moved_scales[:].bitcast(I32), 0)
+        was_rows = wa_scales.bitcast(I32)
+        for q in range(QUADS):
+            nc.sync.dma_start(
+                wa_plane[QUAD * q : QUAD * q + ROWS, :].bitcast(I32).rearrange("r (z c) -> r z c", z=PASSES),
+                was_rows[:, ROWS * q : ROWS * (q + 1), :].rearrange("z r c -> r z c"),
+            )
+
+        spread = ps.tile([P, 2, N // P, P], F32, name="spread")
+        for v in range(2):
+            for c in range(N // P):
+                nc.tensor.transpose(spread[:, v, c, :], cols[v][:, c : c + 1].to_broadcast([P, P]), ident[:])
+        nc.scalar.copy(rows[:].rearrange("j v (p c) -> j v p c", c=N // P), spread[:].rearrange("j v c p -> j v p c"))
+        bias_rows, gain_rows = rows[:, 0, :], rows[:, 1, :]
+
+        for s in range(2):
+            nc.vector.tensor_copy(picked_scales[:, s * J : (s + 1) * J], x_scales[:].indirect(lists[s][:]))
+        live = QUAD * (QUADS - 1) + ROWS
+        nc.sync.dma_start(moved_scales[0:live, :].bitcast(I32), picked_scales[ROWS : ROWS + live, :].bitcast(I32))
+        x_plane = [picked_scales, moved_scales]
+
+        def gather(s, z):
+            nc.vector.tensor_copy(picked[s][z][:], x_words[z][:].indirect(lists[s][:]))
+
+        def quantize(z):
+            nc.vector.quantize_mx(
+                out=wb_codes[z][:].bitcast(E4M3X4),
+                scales=wb_plane[z][:],
+                in_=wb_grouped[z][:].rearrange("p n t -> p (n t)"),
+            )
+
+        acc = [[ps.tile([P, N], F32, name="acc%d%d" % (s, h)) for h in range(SLOT_TILES)] for s in range(2)]
+
+        def product(s, z):
+            for h in range(SLOT_TILES):
+                if s == 0:
+                    codes, plane = wa_codes[:, z, :], wa_plane[:, z * N : (z + 1) * N]
+                else:
+                    codes, plane = wb_codes[z][:], wb_plane[z][:]
+                nc.tensor.matmul_mx(
+                    out=acc[s][h][:],
+                    lhsT=picked[s][z][:, h * P : (h + 1) * P].bitcast(E5M2X4),
+                    lhsT_scale=x_plane[z][:, s * J + h * P : s * J + (h + 1) * P],
+                    rhs=codes.bitcast(E4M3X4),
+                    rhs_scale=plane,
+                    start=(z == 0),
+                    stop=(z == PASSES - 1),
+                )
+
+        gather(1, 0)
+        gather(0, 0)
+        round_and_interleave(nc.scalar.copy, wb_grouped[0], wb_raw[0], 0, N)
+        gather(1, 1)
+        quantize(0)
+        product(1, 0)
+        gather(0, 1)
+        round_and_interleave(nc.scalar.copy, wb_grouped[1], wb_raw[1], VECTOR_COLS, N)
+        round_and_interleave(nc.vector.tensor_copy, wb_grouped[1], wb_raw[1], 0, VECTOR_COLS)
+        quantize(1)
+        product(0, 0)
+        product(0, 1)
+        product(1, 1)
+
+        less_bias = [sb.tile([P, N], F32, name="less_bias%d" % h) for h in range(SLOT_TILES)]
+        squares = [sb.tile([P, N + 1], F32, name="squares%d" % h) for h in range(SLOT_TILES)]
+        denom = [sb.tile([P, 1], F32, name="denom%d" % h) for h in range(SLOT_TILES)]
+        recip = [sb.tile([P, 1], F32, name="recip%d" % h) for h in range(SLOT_TILES)]
+        result = [sb.tile([P, N], F32, name="result%d" % h) for h in range(SLOT_TILES)]
+        for h in range(SLOT_TILES):
+            nc.vector.tensor_tensor(less_bias[h][:], acc[0][h][:], bias_rows, ALU.subtract)
+        for h in range(SLOT_TILES):
+            nc.vector.tensor_tensor(gap[:, h, 0:N], acc[1][h][:], less_bias[h][:], ALU.subtract)
+            nc.scalar.activation(squares[h][:], gap[:, h, :], ACT.Square, scale=1.0 / math.sqrt(N), accum_out=denom[h][:])
+        for h in range(SLOT_TILES):
+            nc.vector.reciprocal(recip[h][:], denom[h][:])
+            nc.vector.scalar_tensor_tensor(result[h][:], acc[0][h][:], recip[h][:], gain_rows, ALU.mult, ALU.mult)
+            nc.sync.dma_start(out[h * P : (h + 1) * P, :], result[h][:])

@@ -26,7 +26,7 @@ QUAD = P // QUADS
 ROWS = 4
 SLOT_TILES = J // P
 GAP_FLOOR = 0.4
-VECTOR_COLS = 144
+VECTOR_COLS = 160
 
 
 def round_and_interleave(copy, grouped, raw, c0, c1):
@@ -40,83 +40,94 @@ def tile_list_rows_twotokens_bygapsize_kernel(tc, xt_words, xt_scales, wa_words,
     nc = tc.nc
     with ExitStack() as ctx:
         sb = ctx.enter_context(tc.tile_pool(name="sb", bufs=1))
-        late = ctx.enter_context(tc.tile_pool(name="late", bufs=1))
         ps = ctx.enter_context(tc.psum_pool(name="ps", bufs=1))
 
         lists = [sb.tile([P, J // 16], U16, name="list%d" % s) for s in range(2)]
-        ramp = late.tile([P, QUAD], F32, name="ramp", align_bytes=64, offset=4 * T - 64)
-        ramp_t = late.tile([P, QUAD], F32, name="ramp_t", align_bytes=64, offset=4 * T + 4 * PACK * N)
-        x_words = [
-            sb.tile([P, T], U32, name="x_words0", align_bytes=64),
-            late.tile([P, T], U32, name="x_words1", align_bytes=64, offset=0),
-        ]
-        x_scales = sb.tile([P, T], U8, name="x_scales", align_bytes=64)
-        wa_codes = late.tile([P, PASSES, N], U32, name="wa_codes", align_bytes=64, offset=4 * T + 64 + 4 * PACK * N)
+        x_words = [sb.tile([P, T], U32, name="x_words%d" % z, align_bytes=64) for z in range(PASSES)]
+        x_scales = sb.tile([P, T], U8, name="x_scales", tag="shared", align_bytes=64)
         wa_plane = sb.tile([P, PASSES * N], U8, name="wa_plane", align_bytes=64)
-        wb_raw = [
-            sb.tile([P, PACK, N], F32, name="wb_raw0"),
-            late.tile([P, PACK, N], F32, name="wb_raw1", align_bytes=64, offset=4 * T + 64),
-        ]
         wb_grouped = [sb.tile([P, N, PACK], BF16, name="wb_grouped%d" % z, align_bytes=64) for z in range(PASSES)]
         wb_codes = [sb.tile([P, N], U32, name="wb_codes%d" % z, align_bytes=64) for z in range(PASSES)]
         wb_plane = [sb.tile([P, N], U8, name="wb_plane%d" % z, align_bytes=64) for z in range(PASSES)]
         picked_scales = sb.tile([P, 2 * J], U8, name="picked_scales", align_bytes=64)
         moved_scales = sb.tile([P, 2 * J], U8, name="moved_scales", align_bytes=64)
-        picked = [[sb.tile([P, J], U32, name="picked%d%d" % (s, z), align_bytes=64) for z in range(PASSES)] for s in range(2)]
-        cols = [late.tile([P, N // P], F32, name="cols%d" % v, offset=4 * T + 32 * v) for v in range(2)]
-        rows = sb.tile([P, 2, N], F32, name="rows")
+        picked_second = sb.tile([P, 2, J], U32, name="picked1", align_bytes=64)
+        wa_codes = sb.tile([P, PASSES, N], U32, name="wa_codes", align_bytes=64)
+        cols = [sb.tile([P, N // P], F32, name="cols%d" % v) for v in range(2)]
         ident = sb.tile([P, P], F32, name="ident")
-        ones = sb.tile([P, QUAD], F32, name="ones")
+        ones = sb.tile([P, QUAD], F32, name="ones", tag="wb_raw0")
+        unit = sb.tile([P, SLOT_TILES], F32, name="unit")
+        ramp = sb.tile([P, QUAD], F32, name="ramp", align_bytes=64)
+        ramp_t = sb.tile([P, QUAD], F32, name="ramp_t", align_bytes=64)
         gap = sb.tile([P, SLOT_TILES, N + 1], F32, name="gap")
 
-        nc.vector.memset(x_scales[:].bitcast(I32), 0)
-        nc.sync.dma_start(lists[0][:], offs)
-        nc.scalar.dma_start(x_words[0][:].bitcast(I32), xt_words[0].rearrange("p n t -> p (n t)").bitcast(I32))
-        nc.sync.dma_start(lists[1][:], offs2)
-        nc.scalar.dma_start(wb_raw[0][:], wb[0:K_PASS, :].rearrange("(p t) n -> p t n", t=PACK))
         xs_rows = xt_scales.bitcast(I32)
-        for q in range(QUADS):
-            nc.sync.dma_start(
+        was_rows = wa_scales.bitcast(I32)
+
+        def load_words(queue, z):
+            queue.dma_start(x_words[z][:].bitcast(I32), xt_words[z].rearrange("p n t -> p (n t)").bitcast(I32))
+
+        def load_wb(queue, z):
+            queue.dma_start(wb_raw[z][:], wb[z * K_PASS : (z + 1) * K_PASS, :].rearrange("(p t) n -> p t n", t=PACK))
+
+        def load_x_scales(queue, q):
+            queue.dma_start(
                 x_scales[QUAD * q : QUAD * q + PASSES * ROWS, :].bitcast(I32), xs_rows[:, ROWS * q : ROWS * (q + 1), :]
             )
-        nc.vector.memset(ones[:], 1.0)
-        nc.scalar.activation(gap[:, :, N], ones[:, 0:SLOT_TILES], ACT.Copy, scale=math.sqrt(GAP_FLOOR * N))
-        nc.vector.tensor_tensor_scan(ramp[:], ones[:], ones[:], 0.0, ALU.mult, ALU.add)
-        nc.vector.memset(ident[:], 0.0)
-        nc.vector.transpose(ramp_t[:], ramp[:])
-        for q in range(QUADS):
-            quad = slice(QUAD * q, QUAD * (q + 1))
-            nc.vector.tensor_tensor(ident[quad, quad], ramp[quad, :], ramp_t[quad, :], ALU.is_equal)
-        nc.scalar.dma_start(x_words[1][:].bitcast(I32), xt_words[1].rearrange("p n t -> p (n t)").bitcast(I32))
-        for v, vec in enumerate((bi, gm)):
-            nc.scalar.dma_start(cols[v][:], vec.rearrange("o (p c) -> (o p) c", c=N // P))
-        nc.scalar.dma_start(wb_raw[1][:], wb[K_PASS:K, :].rearrange("(p t) n -> p t n", t=PACK))
-        nc.scalar.dma_start(wa_codes[:].bitcast(I32), wa_words.rearrange("z p n t -> p z (n t)").bitcast(I32))
 
-        nc.vector.memset(wa_plane[:].bitcast(I32), 0)
-        nc.vector.memset(moved_scales[:].bitcast(I32), 0)
-        was_rows = wa_scales.bitcast(I32)
-        for q in range(QUADS):
-            nc.sync.dma_start(
+        def load_wa_scales(queue, q):
+            queue.dma_start(
                 wa_plane[QUAD * q : QUAD * q + ROWS, :].bitcast(I32).rearrange("r (z c) -> r z c", z=PASSES),
                 was_rows[:, ROWS * q : ROWS * (q + 1), :].rearrange("z r c -> r z c"),
             )
+
+        def load_cols(queue, v, vec):
+            queue.dma_start(cols[v][:], vec.rearrange("o (p c) -> (o p) c", c=N // P))
+
+        nc.vector.memset(x_scales[:].bitcast(I32), 0)
+        nc.vector.memset(ones[:], 1.0)
+        nc.vector.tensor_tensor_scan(ramp[:], ones[:], ones[:], 0.0, ALU.mult, ALU.add)
+        nc.vector.memset(unit[:], 1.0)
+        nc.vector.memset(wa_plane[:].bitcast(I32), 0)
+        wb_raw = [sb.tile([P, PACK, N], F32, name="wb_raw%d" % z, tag="wb_raw%d" % z) for z in range(PASSES)]
+        load_words(nc.scalar, 0)
+        nc.sync.dma_start(lists[0][:], offs)
+        nc.sync.dma_start(lists[1][:], offs2)
+        load_cols(nc.gpsimd, 0, bi)
+        load_cols(nc.gpsimd, 1, gm)
+        load_x_scales(nc.scalar, 3)
+        load_x_scales(nc.sync, 0)
+        load_wb(nc.scalar, 0)
+        load_x_scales(nc.sync, 1)
+        load_x_scales(nc.sync, 2)
+        nc.scalar.activation(gap[:, :, N], unit[:], ACT.Copy, scale=math.sqrt(GAP_FLOOR * N))
+        load_words(nc.sync, 1)
+        nc.sync.dma_start(wa_codes[:].bitcast(I32), wa_words.rearrange("z p n t -> p z (n t)").bitcast(I32))
+        load_wb(nc.sync, 1)
+        for q in range(QUADS):
+            load_wa_scales(nc.scalar, q)
+
+        nc.vector.memset(ident[:], 0.0)
+        nc.vector.transpose(ramp_t[:], ramp[:])
+        nc.vector.memset(moved_scales[:].bitcast(I32), 0)
+        for q in range(QUADS):
+            quad = slice(QUAD * q, QUAD * (q + 1))
+            nc.vector.tensor_tensor(ident[quad, quad], ramp[quad, :], ramp_t[quad, :], ALU.is_equal)
 
         spread = ps.tile([P, 2, N // P, P], F32, name="spread")
         for v in range(2):
             for c in range(N // P):
                 nc.tensor.transpose(spread[:, v, c, :], cols[v][:, c : c + 1].to_broadcast([P, P]), ident[:])
-        nc.scalar.copy(rows[:].rearrange("j v (p c) -> j v p c", c=N // P), spread[:].rearrange("j v c p -> j v p c"))
-        bias_rows, gain_rows = rows[:, 0, :], rows[:, 1, :]
 
         for s in range(2):
             nc.vector.tensor_copy(picked_scales[:, s * J : (s + 1) * J], x_scales[:].indirect(lists[s][:]))
         live = QUAD * (QUADS - 1) + ROWS
         nc.sync.dma_start(moved_scales[0:live, :].bitcast(I32), picked_scales[ROWS : ROWS + live, :].bitcast(I32))
         x_plane = [picked_scales, moved_scales]
+        picked = [sb.tile([P, 2, J], U32, name="picked0", tag="shared", align_bytes=64), picked_second]
 
         def gather(s, z):
-            nc.vector.tensor_copy(picked[s][z][:], x_words[z][:].indirect(lists[s][:]))
+            nc.vector.tensor_copy(picked[z][:, s, :], x_words[z][:].indirect(lists[s][:]))
 
         def quantize(z):
             nc.vector.quantize_mx(
@@ -135,7 +146,7 @@ def tile_list_rows_twotokens_bygapsize_kernel(tc, xt_words, xt_scales, wa_words,
                     codes, plane = wb_codes[z][:], wb_plane[z][:]
                 nc.tensor.matmul_mx(
                     out=acc[s][h][:],
-                    lhsT=picked[s][z][:, h * P : (h + 1) * P].bitcast(E5M2X4),
+                    lhsT=picked[z][:, s, h * P : (h + 1) * P].bitcast(E5M2X4),
                     lhsT_scale=x_plane[z][:, s * J + h * P : s * J + (h + 1) * P],
                     rhs=codes.bitcast(E4M3X4),
                     rhs_scale=plane,
@@ -143,18 +154,21 @@ def tile_list_rows_twotokens_bygapsize_kernel(tc, xt_words, xt_scales, wa_words,
                     stop=(z == PASSES - 1),
                 )
 
-        gather(1, 0)
         gather(0, 0)
+        gather(1, 0)
         round_and_interleave(nc.scalar.copy, wb_grouped[0], wb_raw[0], 0, N)
-        gather(1, 1)
+        rows = sb.tile([P, 2, N], F32, name="rows", tag="wb_raw0")
+        nc.scalar.copy(rows[:].rearrange("j v (p c) -> j v p c", c=N // P), spread[:].rearrange("j v c p -> j v p c"))
+        bias_rows, gain_rows = rows[:, 0, :], rows[:, 1, :]
+        product(0, 0)
+        gather(0, 1)
         quantize(0)
         product(1, 0)
-        gather(0, 1)
+        gather(1, 1)
+        product(0, 1)
         round_and_interleave(nc.scalar.copy, wb_grouped[1], wb_raw[1], VECTOR_COLS, N)
         round_and_interleave(nc.vector.tensor_copy, wb_grouped[1], wb_raw[1], 0, VECTOR_COLS)
         quantize(1)
-        product(0, 0)
-        product(0, 1)
         product(1, 1)
 
         less_bias = [sb.tile([P, N], F32, name="less_bias%d" % h) for h in range(SLOT_TILES)]
@@ -162,12 +176,17 @@ def tile_list_rows_twotokens_bygapsize_kernel(tc, xt_words, xt_scales, wa_words,
         denom = [sb.tile([P, 1], F32, name="denom%d" % h) for h in range(SLOT_TILES)]
         recip = [sb.tile([P, 1], F32, name="recip%d" % h) for h in range(SLOT_TILES)]
         result = [sb.tile([P, N], F32, name="result%d" % h) for h in range(SLOT_TILES)]
+        gained = sb.tile([P, N], F32, name="gained")
         for h in range(SLOT_TILES):
             nc.vector.tensor_tensor(less_bias[h][:], acc[0][h][:], bias_rows, ALU.subtract)
+        nc.vector.tensor_tensor(gained[:], acc[0][0][:], gain_rows, ALU.mult)
         for h in range(SLOT_TILES):
             nc.vector.tensor_tensor(gap[:, h, 0:N], acc[1][h][:], less_bias[h][:], ALU.subtract)
-            nc.scalar.activation(squares[h][:], gap[:, h, :], ACT.Square, scale=1.0 / math.sqrt(N), accum_out=denom[h][:])
+        nc.scalar.activation(squares[0][:], gap[:, 0, :], ACT.Square, scale=1.0 / math.sqrt(N), accum_out=denom[0][:])
+        nc.vector.scalar_tensor_tensor(squares[1][:], gap[:, 1, :], 1.0 / N, gap[:, 1, :], ALU.mult, ALU.mult, accum_out=denom[1][:])
         for h in range(SLOT_TILES):
             nc.vector.reciprocal(recip[h][:], denom[h][:])
-            nc.vector.scalar_tensor_tensor(result[h][:], acc[0][h][:], recip[h][:], gain_rows, ALU.mult, ALU.mult)
-            nc.sync.dma_start(out[h * P : (h + 1) * P, :], result[h][:])
+        nc.scalar.activation(result[0][:], gained[:], ACT.Copy, scale=recip[0][:])
+        nc.vector.scalar_tensor_tensor(result[1][:], acc[0][1][:], recip[1][:], gain_rows, ALU.mult, ALU.mult)
+        nc.scalar.dma_start(out[0:P, :], result[0][:])
+        nc.sync.dma_start(out[P : 2 * P, :], result[1][:])

@@ -26,7 +26,7 @@ QUAD = P // QUADS
 ROWS = 4
 SLOT_TILES = J // P
 GAP_FLOOR = 0.4
-VECTOR_COLS = 160
+VECTOR_COLS = 176
 
 
 def round_and_interleave(copy, grouped, raw, c0, c1):
@@ -90,17 +90,16 @@ def tile_list_rows_twotokens_bygapsize_kernel(tc, xt_words, xt_scales, wa_words,
         nc.vector.memset(unit[:], 1.0)
         nc.vector.memset(wa_plane[:].bitcast(I32), 0)
         wb_raw = [sb.tile([P, PACK, N], F32, name="wb_raw%d" % z, tag="wb_raw%d" % z) for z in range(PASSES)]
-        load_words(nc.scalar, 0)
         nc.sync.dma_start(lists[0][:], offs)
         nc.sync.dma_start(lists[1][:], offs2)
-        load_cols(nc.gpsimd, 0, bi)
-        load_cols(nc.gpsimd, 1, gm)
-        load_x_scales(nc.scalar, 3)
+        load_words(nc.sync, 0)
         load_x_scales(nc.sync, 0)
-        load_wb(nc.scalar, 0)
-        load_x_scales(nc.sync, 1)
-        load_x_scales(nc.sync, 2)
+        for q in range(1, QUADS):
+            load_x_scales(nc.scalar, q)
+        load_wb(nc.sync, 0)
         nc.scalar.activation(gap[:, :, N], unit[:], ACT.Copy, scale=math.sqrt(GAP_FLOOR * N))
+        load_cols(nc.sync, 0, bi)
+        load_cols(nc.sync, 1, gm)
         load_words(nc.sync, 1)
         nc.sync.dma_start(wa_codes[:].bitcast(I32), wa_words.rearrange("z p n t -> p z (n t)").bitcast(I32))
         load_wb(nc.sync, 1)

@@ -44,19 +44,17 @@ def tile_list_rows_twotokens_bygapsize_kernel(tc, xt_words, xt_scales, wa_words,
 
         lists = [sb.tile([P, J // 16], U16, name="list%d" % s) for s in range(2)]
         x_words = [sb.tile([P, T], U32, name="x_words%d" % z, align_bytes=64) for z in range(PASSES)]
-        x_scales = sb.tile([P, T], U8, name="x_scales", tag="shared", align_bytes=64)
+        x_scales = sb.tile([P, T], U8, name="x_scales", align_bytes=64)
         wa_plane = sb.tile([P, PASSES * N], U8, name="wa_plane", align_bytes=64)
-        wb_grouped = [sb.tile([P, N, PACK], BF16, name="wb_grouped%d" % z, align_bytes=64) for z in range(PASSES)]
+        wb_grouped = [sb.tile([P, N, PACK], BF16, name="wb_grouped%d" % z, tag="wb_grouped%d" % z, align_bytes=64) for z in range(PASSES)]
         wb_codes = [sb.tile([P, N], U32, name="wb_codes%d" % z, align_bytes=64) for z in range(PASSES)]
         wb_plane = [sb.tile([P, N], U8, name="wb_plane%d" % z, align_bytes=64) for z in range(PASSES)]
         picked_scales = sb.tile([P, 2 * J], U8, name="picked_scales", align_bytes=64)
         moved_scales = sb.tile([P, 2 * J], U8, name="moved_scales", align_bytes=64)
-        picked_second = sb.tile([P, 2, J], U32, name="picked1", align_bytes=64)
         wa_codes = sb.tile([P, PASSES, N], U32, name="wa_codes", align_bytes=64)
         cols = [sb.tile([P, N // P], F32, name="cols%d" % v) for v in range(2)]
         ident = sb.tile([P, P], F32, name="ident")
-        ones = sb.tile([P, QUAD], F32, name="ones", tag="wb_raw0")
-        unit = sb.tile([P, SLOT_TILES], F32, name="unit")
+        ones = sb.tile([P, QUAD], F32, name="ones")
         ramp = sb.tile([P, QUAD], F32, name="ramp", align_bytes=64)
         ramp_t = sb.tile([P, QUAD], F32, name="ramp_t", align_bytes=64)
         gap = sb.tile([P, SLOT_TILES, N + 1], F32, name="gap")
@@ -87,24 +85,22 @@ def tile_list_rows_twotokens_bygapsize_kernel(tc, xt_words, xt_scales, wa_words,
         nc.vector.memset(x_scales[:].bitcast(I32), 0)
         nc.vector.memset(ones[:], 1.0)
         nc.vector.tensor_tensor_scan(ramp[:], ones[:], ones[:], 0.0, ALU.mult, ALU.add)
-        nc.vector.memset(unit[:], 1.0)
         nc.vector.memset(wa_plane[:].bitcast(I32), 0)
         wb_raw = [sb.tile([P, PACK, N], F32, name="wb_raw%d" % z, tag="wb_raw%d" % z) for z in range(PASSES)]
+        load_words(nc.scalar, 0)
         nc.sync.dma_start(lists[0][:], offs)
         nc.sync.dma_start(lists[1][:], offs2)
-        load_words(nc.sync, 0)
-        load_x_scales(nc.sync, 0)
-        for q in range(1, QUADS):
-            load_x_scales(nc.scalar, q)
-        load_wb(nc.sync, 0)
-        nc.scalar.activation(gap[:, :, N], unit[:], ACT.Copy, scale=math.sqrt(GAP_FLOOR * N))
+        load_wb(nc.scalar, 0)
+        for q in range(QUADS):
+            load_x_scales(nc.sync, q)
+        nc.scalar.activation(gap[:, :, N], ones[:, 0:SLOT_TILES], ACT.Copy, scale=math.sqrt(GAP_FLOOR * N))
         load_cols(nc.sync, 0, bi)
         load_cols(nc.sync, 1, gm)
-        load_words(nc.sync, 1)
-        nc.sync.dma_start(wa_codes[:].bitcast(I32), wa_words.rearrange("z p n t -> p z (n t)").bitcast(I32))
-        load_wb(nc.sync, 1)
+        load_words(nc.scalar, 1)
+        nc.scalar.dma_start(wa_codes[:].bitcast(I32), wa_words.rearrange("z p n t -> p z (n t)").bitcast(I32))
+        load_wb(nc.scalar, 1)
         for q in range(QUADS):
-            load_wa_scales(nc.scalar, q)
+            load_wa_scales(nc.sync, q)
 
         nc.vector.memset(ident[:], 0.0)
         nc.vector.transpose(ramp_t[:], ramp[:])
@@ -123,10 +119,14 @@ def tile_list_rows_twotokens_bygapsize_kernel(tc, xt_words, xt_scales, wa_words,
         live = QUAD * (QUADS - 1) + ROWS
         nc.sync.dma_start(moved_scales[0:live, :].bitcast(I32), picked_scales[ROWS : ROWS + live, :].bitcast(I32))
         x_plane = [picked_scales, moved_scales]
-        picked = [sb.tile([P, 2, J], U32, name="picked0", tag="shared", align_bytes=64), picked_second]
+        picked = {
+            (s, z): sb.tile([P, J], U32, name="picked%d%d" % (s, z), align_bytes=64)
+            for s in range(2)
+            for z in range(PASSES)
+        }
 
         def gather(s, z):
-            nc.vector.tensor_copy(picked[z][:, s, :], x_words[z][:].indirect(lists[s][:]))
+            nc.vector.tensor_copy(picked[s, z][:], x_words[z][:].indirect(lists[s][:]))
 
         def quantize(z):
             nc.vector.quantize_mx(
@@ -145,7 +145,7 @@ def tile_list_rows_twotokens_bygapsize_kernel(tc, xt_words, xt_scales, wa_words,
                     codes, plane = wb_codes[z][:], wb_plane[z][:]
                 nc.tensor.matmul_mx(
                     out=acc[s][h][:],
-                    lhsT=picked[z][:, s, h * P : (h + 1) * P].bitcast(E5M2X4),
+                    lhsT=picked[s, z][:, h * P : (h + 1) * P].bitcast(E5M2X4),
                     lhsT_scale=x_plane[z][:, s * J + h * P : s * J + (h + 1) * P],
                     rhs=codes.bitcast(E4M3X4),
                     rhs_scale=plane,
@@ -159,10 +159,10 @@ def tile_list_rows_twotokens_bygapsize_kernel(tc, xt_words, xt_scales, wa_words,
         rows = sb.tile([P, 2, N], F32, name="rows", tag="wb_raw0")
         nc.scalar.copy(rows[:].rearrange("j v (p c) -> j v p c", c=N // P), spread[:].rearrange("j v c p -> j v p c"))
         bias_rows, gain_rows = rows[:, 0, :], rows[:, 1, :]
-        product(0, 0)
-        gather(0, 1)
         quantize(0)
         product(1, 0)
+        product(0, 0)
+        gather(0, 1)
         gather(1, 1)
         product(0, 1)
         round_and_interleave(nc.scalar.copy, wb_grouped[1], wb_raw[1], VECTOR_COLS, N)
@@ -170,17 +170,17 @@ def tile_list_rows_twotokens_bygapsize_kernel(tc, xt_words, xt_scales, wa_words,
         quantize(1)
         product(1, 1)
 
-        less_bias = [sb.tile([P, N], F32, name="less_bias%d" % h) for h in range(SLOT_TILES)]
+        less_bias = sb.tile([P, SLOT_TILES, N], F32, name="less_bias", tag="wb_grouped1", align_bytes=64)
         squares = [sb.tile([P, N + 1], F32, name="squares%d" % h) for h in range(SLOT_TILES)]
         denom = [sb.tile([P, 1], F32, name="denom%d" % h) for h in range(SLOT_TILES)]
         recip = [sb.tile([P, 1], F32, name="recip%d" % h) for h in range(SLOT_TILES)]
         result = [sb.tile([P, N], F32, name="result%d" % h) for h in range(SLOT_TILES)]
-        gained = sb.tile([P, N], F32, name="gained")
+        gained = sb.tile([P, N], F32, name="gained", tag="wb_raw1")
         for h in range(SLOT_TILES):
-            nc.vector.tensor_tensor(less_bias[h][:], acc[0][h][:], bias_rows, ALU.subtract)
+            nc.vector.tensor_tensor(less_bias[:, h, :], acc[0][h][:], bias_rows, ALU.subtract)
         nc.vector.tensor_tensor(gained[:], acc[0][0][:], gain_rows, ALU.mult)
         for h in range(SLOT_TILES):
-            nc.vector.tensor_tensor(gap[:, h, 0:N], acc[1][h][:], less_bias[h][:], ALU.subtract)
+            nc.vector.tensor_tensor(gap[:, h, 0:N], acc[1][h][:], less_bias[:, h, :], ALU.subtract)
         nc.scalar.activation(squares[0][:], gap[:, 0, :], ACT.Square, scale=1.0 / math.sqrt(N), accum_out=denom[0][:])
         nc.vector.scalar_tensor_tensor(squares[1][:], gap[:, 1, :], 1.0 / N, gap[:, 1, :], ALU.mult, ALU.mult, accum_out=denom[1][:])
         for h in range(SLOT_TILES):

import math
from contextlib import ExitStack

import concourse.mybir as mybir

K, T, J, N = 1024, 1024, 256, 256
FLOPS = 2 * 2 * K * J * N

F32 = mybir.dt.float32
BF16 = mybir.dt.bfloat16
I32 = mybir.dt.int32
U32 = mybir.dt.uint32
U16 = mybir.dt.uint16
U8 = mybir.dt.uint8
E4M3X4 = mybir.dt.float8_e4m3fn_x4
E5M2X4 = mybir.dt.float8_e5m2_x4
ALU = mybir.AluOpType
ACT = mybir.ActivationFunctionType

P = 128
PACK = 4
K_PASS = P * PACK
PASSES = K // K_PASS
QUADS = 4
QUAD = P // QUADS
ROWS = 4
SLOT_TILES = J // P
GAP_FLOOR = 0.4
VECTOR_COLS = 176


def round_and_interleave(copy, grouped, raw, c0, c1):
    copy(
        grouped[:, c0:c1, :].rearrange("p (c i) t -> p c t i", i=4),
        raw[:, :, c0:c1].rearrange("p t (c i) -> p c t i", i=4),
    )


def tile_list_rows_twotokens_bygapsize_kernel(tc, xt_words, xt_scales, wa_words, wa_scales, wb, bi, gm, offs, offs2, out):
    nc = tc.nc
    with ExitStack() as ctx:
        sb = ctx.enter_context(tc.tile_pool(name="sb", bufs=1))
        ps = ctx.enter_context(tc.psum_pool(name="ps", bufs=1))

        lists = [sb.tile([P, J // 16], U16, name="list%d" % s) for s in range(2)]
        x_words = [sb.tile([P, T], U32, name="x_words%d" % z, align_bytes=64) for z in range(PASSES)]
        x_scales = sb.tile([P, T], U8, name="x_scales", align_bytes=64)
        wa_plane = sb.tile([P, PASSES * N], U8, name="wa_plane", align_bytes=64)
        wb_grouped = [sb.tile([P, N, PACK], BF16, name="wb_grouped%d" % z, tag="wb_grouped%d" % z, align_bytes=64) for z in range(PASSES)]
        wb_codes = [sb.tile([P, N], U32, name="wb_codes%d" % z, align_bytes=64) for z in range(PASSES)]
        wb_plane = [sb.tile([P, N], U8, name="wb_plane%d" % z, align_bytes=64) for z in range(PASSES)]
        picked_scales = sb.tile([P, 2 * J], U8, name="picked_scales", align_bytes=64)
        moved_scales = sb.tile([P, 2 * J], U8, name="moved_scales", align_bytes=64)
        wa_codes = sb.tile([P, PASSES, N], U32, name="wa_codes", align_bytes=64)
        cols = [sb.tile([P, N // P], F32, name="cols%d" % v) for v in range(2)]
        ident = sb.tile([P, P], F32, name="ident")
        ones = sb.tile([P, QUAD], F32, name="ones")
        ramp = sb.tile([P, QUAD], F32, name="ramp", align_bytes=64)
        ramp_t = sb.tile([P, QUAD], F32, name="ramp_t", align_bytes=64)
        gap = sb.tile([P, SLOT_TILES, N + 1], F32, name="gap")

        xs_rows = xt_scales.bitcast(I32)
        was_rows = wa_scales.bitcast(I32)

        def load_words(queue, z):
            queue.dma_start(x_words[z][:].bitcast(I32), xt_words[z].rearrange("p n t -> p (n t)").bitcast(I32))

        def load_wb(queue, z):
            queue.dma_start(wb_raw[z][:], wb[z * K_PASS : (z + 1) * K_PASS, :].rearrange("(p t) n -> p t n", t=PACK))

        def load_x_scales(queue, q):
            queue.dma_start(
                x_scales[QUAD * q : QUAD * q + PASSES * ROWS, :].bitcast(I32), xs_rows[:, ROWS * q : ROWS * (q + 1), :]
            )

        def load_wa_scales(queue, q):
            queue.dma_start(
                wa_plane[QUAD * q : QUAD * q + ROWS, :].bitcast(I32).rearrange("r (z c) -> r z c", z=PASSES),
                was_rows[:, ROWS * q : ROWS * (q + 1), :].rearrange("z r c -> r z c"),
            )

        def load_cols(queue, v, vec):
            queue.dma_start(cols[v][:], vec.rearrange("o (p c) -> (o p) c", c=N // P))

        nc.vector.memset(x_scales[:].bitcast(I32), 0)
        nc.vector.memset(ones[:], 1.0)
        nc.vector.tensor_tensor_scan(ramp[:], ones[:], ones[:], 0.0, ALU.mult, ALU.add)
        nc.vector.memset(wa_plane[:].bitcast(I32), 0)
        wb_raw = [sb.tile([P, PACK, N], F32, name="wb_raw%d" % z, tag="wb_raw%d" % z) for z in range(PASSES)]
        load_words(nc.scalar, 0)
        nc.sync.dma_start(lists[0][:], offs)
        nc.sync.dma_start(lists[1][:], offs2)
        load_wb(nc.scalar, 0)
        for q in range(QUADS):
            load_x_scales(nc.sync, q)
        nc.scalar.activation(gap[:, :, N], ones[:, 0:SLOT_TILES], ACT.Copy, scale=math.sqrt(GAP_FLOOR * N))
        load_cols(nc.sync, 0, bi)
        load_cols(nc.sync, 1, gm)
        load_words(nc.scalar, 1)
        nc.scalar.dma_start(wa_codes[:].bitcast(I32), wa_words.rearrange("z p n t -> p z (n t)").bitcast(I32))
        load_wb(nc.scalar, 1)
        for q in range(QUADS):
            load_wa_scales(nc.sync, q)

        nc.vector.memset(ident[:], 0.0)
        nc.vector.transpose(ramp_t[:], ramp[:])
        nc.vector.memset(moved_scales[:].bitcast(I32), 0)
        for q in range(QUADS):
            quad = slice(QUAD * q, QUAD * (q + 1))
            nc.vector.tensor_tensor(ident[quad, quad], ramp[quad, :], ramp_t[quad, :], ALU.is_equal)

        spread = ps.tile([P, 2, N // P, P], F32, name="spread")
        for v in range(2):
            for c in range(N // P):
                nc.tensor.transpose(spread[:, v, c, :], cols[v][:, c : c + 1].to_broadcast([P, P]), ident[:])

        for s in range(2):
            nc.vector.tensor_copy(picked_scales[:, s * J : (s + 1) * J], x_scales[:].indirect(lists[s][:]))
        live = QUAD * (QUADS - 1) + ROWS
        nc.sync.dma_start(moved_scales[0:live, :].bitcast(I32), picked_scales[ROWS : ROWS + live, :].bitcast(I32))
        x_plane = [picked_scales, moved_scales]
        picked = {
            (s, z): sb.tile([P, J], U32, name="picked%d%d" % (s, z), align_bytes=64)
            for s in range(2)
            for z in range(PASSES)
        }

        def gather(s, z):
            nc.vector.tensor_copy(picked[s, z][:], x_words[z][:].indirect(lists[s][:]))

        def quantize(z):
            nc.vector.quantize_mx(
                out=wb_codes[z][:].bitcast(E4M3X4),
                scales=wb_plane[z][:],
                in_=wb_grouped[z][:].rearrange("p n t -> p (n t)"),
            )

        acc = [[ps.tile([P, N], F32, name="acc%d%d" % (s, h)) for h in range(SLOT_TILES)] for s in range(2)]

        def product(s, z):
            for h in range(SLOT_TILES):
                if s == 0:
                    codes, plane = wa_codes[:, z, :], wa_plane[:, z * N : (z + 1) * N]
                else:
                    codes, plane = wb_codes[z][:], wb_plane[z][:]
                nc.tensor.matmul_mx(
                    out=acc[s][h][:],
                    lhsT=picked[s, z][:, h * P : (h + 1) * P].bitcast(E5M2X4),
                    lhsT_scale=x_plane[z][:, s * J + h * P : s * J + (h + 1) * P],
                    rhs=codes.bitcast(E4M3X4),
                    rhs_scale=plane,
                    start=(z == 0),
                    stop=(z == PASSES - 1),
                )

        gather(0, 0)
        gather(1, 0)
        round_and_interleave(nc.scalar.copy, wb_grouped[0], wb_raw[0], 0, N)
        rows = sb.tile([P, 2, N], F32, name="rows", tag="wb_raw0")
        nc.scalar.copy(rows[:].rearrange("j v (p c) -> j v p c", c=N // P), spread[:].rearrange("j v c p -> j v p c"))
        bias_rows, gain_rows = rows[:, 0, :], rows[:, 1, :]
        quantize(0)
        product(1, 0)
        product(0, 0)
        gather(0, 1)
        gather(1, 1)
        product(0, 1)
        round_and_interleave(nc.scalar.copy, wb_grouped[1], wb_raw[1], VECTOR_COLS, N)
        round_and_interleave(nc.vector.tensor_copy, wb_grouped[1], wb_raw[1], 0, VECTOR_COLS)
        quantize(1)
        product(1, 1)

        less_bias = sb.tile([P, SLOT_TILES, N], F32, name="less_bias", tag="wb_grouped1", align_bytes=64)
        squares = [sb.tile([P, N + 1], F32, name="squares%d" % h) for h in range(SLOT_TILES)]
        denom = [sb.tile([P, 1], F32, name="denom%d" % h) for h in range(SLOT_TILES)]
        recip = [sb.tile([P, 1], F32, name="recip%d" % h) for h in range(SLOT_TILES)]
        result = [sb.tile([P, N], F32, name="result%d" % h) for h in range(SLOT_TILES)]
        gained = sb.tile([P, N], F32, name="gained", tag="wb_raw1")
        for h in range(SLOT_TILES):
            nc.vector.tensor_tensor(less_bias[:, h, :], acc[0][h][:], bias_rows, ALU.subtract)
        nc.vector.tensor_tensor(gained[:], acc[0][0][:], gain_rows, ALU.mult)
        for h in range(SLOT_TILES):
            nc.vector.tensor_tensor(gap[:, h, 0:N], acc[1][h][:], less_bias[:, h, :], ALU.subtract)
        nc.scalar.activation(squares[0][:], gap[:, 0, :], ACT.Square, scale=1.0 / math.sqrt(N), accum_out=denom[0][:])
        nc.vector.scalar_tensor_tensor(squares[1][:], gap[:, 1, :], 1.0 / N, gap[:, 1, :], ALU.mult, ALU.mult, accum_out=denom[1][:])
        for h in range(SLOT_TILES):
            nc.vector.reciprocal(recip[h][:], denom[h][:])
        nc.scalar.activation(result[0][:], gained[:], ACT.Copy, scale=recip[0][:])
        nc.vector.scalar_tensor_tensor(result[1][:], acc[0][1][:], recip[1][:], gain_rows, ALU.mult, ALU.mult)
        nc.scalar.dma_start(out[0:P, :], result[0][:])
        nc.sync.dma_start(out[P : 2 * P, :], result[1][:])
